import numpy as np
import ml_dtypes


def mxq(x, axis, fmt="e4m3"):
    dtype, down = {"e4m3": (ml_dtypes.float8_e4m3fn, 7), "e5m2": (ml_dtypes.float8_e5m2, 14)}[fmt]
    v = np.moveaxis(np.asarray(x, np.float32).astype(ml_dtypes.bfloat16).astype(np.float64), axis, -1)
    blocks = v.reshape(v.shape[:-1] + (-1, 32))
    amax = np.abs(blocks).max(-1, keepdims=True)
    byte = np.maximum(np.where(amax > 0, np.frexp(amax)[1] - 1 + 127, 0) - down, 1)
    scale = np.exp2(byte - 127.0)
    codes = (blocks / scale).astype(np.float32).astype(dtype).astype(np.float64)
    return np.moveaxis((codes * scale).reshape(v.shape), -1, axis)


WIDE = False


def mx_kscale(k):
    if not WIDE:
        return np.ones(k)
    levels = np.array([10, -10, 5, -5, 0])
    if k % 512:
        return np.exp2(np.random.permutation(np.resize(levels, k // 32))).repeat(32)
    a = np.empty((k // 512, 16))
    for p in range(k // 512):
        a[p, :8] = np.random.permutation(np.resize(levels, 8))
        for g in range(8):
            far = levels[np.abs(levels - a[p, g]) >= 10]
            a[p, g + 8] = far[np.random.randint(len(far))]
    return np.exp2(a.ravel()).repeat(32)


def f64(x):
    return np.asarray(x).astype(np.float64)


def striped(idx):
    return np.tile(idx.reshape(-1, 16).T, (8, 1)).astype(np.uint16)


def unstriped(offs):
    return offs[:16].T.reshape(-1).astype(np.int64)


E2M1 = np.array([0.0, 0.5, 1.0, 1.5, 2.0, 3.0, 4.0, 6.0, -0.0, -0.5, -1.0, -1.5, -2.0, -3.0, -4.0, -6.0])


def pack_weight(w, fmt):
    k, n = w.shape
    w = f64(np.asarray(w, np.float32).astype(ml_dtypes.bfloat16)).reshape(k // 32, 32, n)
    amax = np.abs(w).max(1)
    if fmt == "e4m3":
        byte = np.frexp(amax)[1] - 1 + 127 - 7
    else:
        mant, ex = np.frexp(amax / 6.0)
        byte = np.where(mant > 0.5, ex, ex - 1) + 127
    byte = np.clip(np.where(amax > 0, byte, 1), 1, 254)
    scaled = (w * np.exp2(127.0 - byte)[:, None, :]).reshape(k, n).astype(np.float32)
    by_word = np.ascontiguousarray(scaled.reshape(k // 512, 128, 4, n).transpose(0, 1, 3, 2))
    if fmt == "e4m3":
        words = by_word.astype(ml_dtypes.float8_e4m3fn).view(np.uint8)
    else:
        c = by_word.astype(ml_dtypes.float4_e2m1fn).view(np.uint8) & 0xF
        words = (c[..., 0::2] | (c[..., 1::2] << 4)).reshape(k // 512, 128, 2 * n)
    return np.ascontiguousarray(words), np.ascontiguousarray(byte.astype(np.uint8).reshape(k // 512, 16, n))


def unpack_weight(words, scales, fmt):
    g, _, n = scales.shape
    words = np.ascontiguousarray(words).reshape(g, 128, n, -1)
    if fmt == "e4m3":
        vals = words.view(ml_dtypes.float8_e4m3fn).astype(np.float64)
    else:
        nib = np.empty((g, 128, n, 4), np.uint8)
        nib[..., 0::2] = words & 0xF
        nib[..., 1::2] = words >> 4
        vals = E2M1[nib]
    vals = vals * np.repeat(np.exp2(scales.astype(np.float64) - 127.0), 8, axis=1)[..., None]
    return vals.transpose(0, 1, 3, 2).reshape(g * 512, n)


def relu2(v):
    return np.maximum(v, 0.0) ** 2


K, T, E, C, N = 2048, 1024, 4, 128, 256
R = 4


def by_expert(wq, xq):
    return np.concatenate([wq[e].T @ xq[:, e * C:(e + 1) * C] for e in range(E)], axis=1)


def setup_inputs():
    n = np.random.standard_normal
    s = mx_kscale(K)[:, None]
    slot_token = np.concatenate([r * (T // R) + np.random.permutation(T // R)[:C // R] for e in range(E) for r in range(R)])
    x = pack_weight(n((K, T)) * s, "e4m3")
    return {
        "x_words": x[0],
        "x_scales": x[1],
        "w": (n((E, K, N)) / np.sqrt(K) / s[None]).astype(np.float32),
        "b": (0.3 * n((N, E))).astype(np.float32),
        "offs": striped(slot_token),
    }


def reference(x_words, x_scales, w, b, offs):
    idx = unstriped(offs)
    xq = unpack_weight(x_words, x_scales, "e4m3")[:, idx]
    y = by_expert(mxq(f64(w), 1, "e4m3"), xq)
    y = relu2(y + np.repeat(f64(b), C, axis=1))
    return y.reshape(N, E, R, C // R).transpose(0, 2, 1, 3).reshape(N, E * C)

@@ -1,0 +1,112 @@
+from contextlib import ExitStack
+
+import concourse.mybir as mybir
+
+K, T, E, C, N, R = 2048, 1024, 4, 128, 256, 4
+FLOPS = 2 * K * N * E * C
+
+F32 = mybir.dt.float32
+BF16 = mybir.dt.bfloat16
+I32 = mybir.dt.int32
+U32 = mybir.dt.uint32
+U16 = mybir.dt.uint16
+U8 = mybir.dt.uint8
+FP8X4 = mybir.dt.float8_e4m3fn_x4
+ACT = mybir.ActivationFunctionType
+ALU = mybir.AluOpType
+
+P = 128
+PACK = 4
+PASSES = K // (P * PACK)
+SLOTS = E * C
+HALVES = N // P
+U = C // R
+LINE = 4
+
+
+def tile_moe_pke_lin_relu2_kernel(tc, x_words, x_scales, w, b, offs, out):
+    nc = tc.nc
+    with ExitStack() as ctx:
+        keep = ctx.enter_context(tc.tile_pool(name="keep", bufs=1))
+        psum = ctx.enter_context(tc.psum_pool(name="psum", bufs=1))
+
+        offsets = keep.tile([P, SLOTS // 16], U16, name="offsets")
+        nc.sync.dma_start(offsets[:], offs)
+
+        token_scales = keep.tile([P, T], U8, name="token_scales", align_bytes=64)
+        nc.vector.memset(token_scales[:].bitcast(I32), 0)
+        for q in range(4):
+            nc.scalar.dma_start(
+                out=token_scales[32 * q : 32 * q + 16, :].bitcast(I32),
+                in_=x_scales[:, 4 * q : 4 * q + 4, :].bitcast(I32),
+            )
+
+        bias = keep.tile([P, HALVES, E], F32, name="bias")
+        nc.scalar.dma_start(out=bias[:], in_=b.rearrange("(h p) e -> p h e", p=P))
+
+        token_words = []
+        for o in range(PASSES):
+            words = keep.tile([P, T], I32, name="token_words%d" % o, align_bytes=64)
+            nc.sync.dma_start(out=words[:], in_=x_words[o].rearrange("p t r -> p (t r)").bitcast(I32))
+            token_words.append(words)
+
+        raw = {}
+        for e in range(E):
+            for o in range(PASSES):
+                raw[e, o] = keep.tile([P, PACK, N], F32, name="raw%d_%d" % (e, o), align_bytes=64)
+                rows = w[e, o * P * PACK : (o + 1) * P * PACK, :]
+                nc.sync.dma_start(out=raw[e, o][:], in_=rows.rearrange("(p j) n -> p j n", j=PACK))
+
+        slot_words = []
+        for o in range(PASSES):
+            gathered = keep.tile([P, SLOTS], U32, name="slot_words%d" % o, align_bytes=64)
+            nc.vector.tensor_copy(gathered[:], token_words[o][:].bitcast(U32).indirect(offsets[:]))
+            slot_words.append(gathered)
+        slot_scales = keep.tile([P, SLOTS], U8, name="slot_scales", align_bytes=64)
+        nc.vector.tensor_copy(slot_scales[:], token_scales[:].indirect(offsets[:]))
+
+        staged = [keep.tile([P, R, E, U], F32, name="staged%d" % h, align_bytes=64) for h in range(HALVES)]
+        out_view = out.rearrange("(h p) (m e u) -> h p m e u", p=P, m=R, e=E)
+
+        for e in range(E):
+            slots = slice(e * C, (e + 1) * C)
+            acc = [psum.tile([P, C], F32, name="acc%d_%d" % (e, h)) for h in range(HALVES)]
+            for o in range(PASSES):
+                grouped = []
+                for h in range(HALVES):
+                    g = keep.tile([P, P, PACK], BF16, name="grouped%d_%d_%d" % (e, o, h), align_bytes=64)
+                    src = raw[e, o][:, :, h * P : (h + 1) * P].rearrange("p j (c i) -> p c j i", i=LINE)
+                    dst = g[:].rearrange("p (c i) j -> p c j i", i=LINE)
+                    if h == 0:
+                        nc.vector.tensor_copy(out=dst, in_=src)
+                    else:
+                        nc.scalar.copy(out=dst, in_=src)
+                    grouped.append(g)
+                for h in range(HALVES):
+                    codes = keep.tile([P, P], U32, name="codes%d_%d_%d" % (e, o, h), align_bytes=64)
+                    scales = keep.tile([P, P], U8, name="scales%d_%d_%d" % (e, o, h), align_bytes=64)
+                    nc.vector.quantize_mx(
+                        out=codes[:].bitcast(FP8X4),
+                        scales=scales[:],
+                        in_=grouped[h][:].rearrange("p n j -> p (n j)"),
+                    )
+                    nc.tensor.matmul_mx(
+                        out=acc[h][:],
+                        lhsT=codes[:].bitcast(FP8X4),
+                        lhsT_scale=scales[:],
+                        rhs=slot_words[o][:, slots].bitcast(FP8X4),
+                        rhs_scale=slot_scales[4 * o : P, slots],
+                        start=(o == 0),
+                        stop=(o == PASSES - 1),
+                    )
+            for h in range(HALVES):
+                pos = keep.tile([P, R, U], F32, name="pos%d_%d" % (e, h), align_bytes=64)
+                nc.scalar.activation(
+                    out=pos[:].rearrange("p m u -> p (m u)"), in_=acc[h][:], func=ACT.Relu, bias=bias[:, h, e : e + 1]
+                )
+                nc.vector.tensor_tensor(out=staged[h][:, :, e, :], in0=pos[:], in1=pos[:], op=ALU.mult)
+            if e == E - 2:
+                for h in range(HALVES):
+                    nc.sync.dma_start(out=out_view[h][:, :, 0 : E - 1, :], in_=staged[h][:, :, 0 : E - 1, :])
+        for h in range(HALVES):
+            nc.sync.dma_start(out=out_view[h][:, :, E - 1, :], in_=staged[h][:, :, E - 1, :])

@@ -22,12 +22,15 @@ SLOTS = E * C
 HALVES = N // P
 U = C // R
 LINE = 4
+SPLIT = 96
+RING = 3
 
 
 def tile_moe_pke_lin_relu2_kernel(tc, x_words, x_scales, w, b, offs, out):
     nc = tc.nc
     with ExitStack() as ctx:
         keep = ctx.enter_context(tc.tile_pool(name="keep", bufs=1))
+        ring = ctx.enter_context(tc.tile_pool(name="ring", bufs=RING))
         psum = ctx.enter_context(tc.psum_pool(name="psum", bufs=1))
 
         offsets = keep.tile([P, SLOTS // 16], U16, name="offsets")
@@ -65,48 +68,48 @@ def tile_moe_pke_lin_relu2_kernel(tc, x_words, x_scales, w, b, offs, out):
         slot_scales = keep.tile([P, SLOTS], U8, name="slot_scales", align_bytes=64)
         nc.vector.tensor_copy(slot_scales[:], token_scales[:].indirect(offsets[:]))
 
-        staged = [keep.tile([P, R, E, U], F32, name="staged%d" % h, align_bytes=64) for h in range(HALVES)]
+        staged = keep.tile([P, HALVES, R, E, U], F32, name="staged", align_bytes=64)
         out_view = out.rearrange("(h p) (m e u) -> h p m e u", p=P, m=R, e=E)
+
+        def interleave(engine_copy, dst, src, lo, hi):
+            engine_copy(
+                out=dst[:, lo:hi, :].rearrange("p (c i) j -> p c j i", i=LINE),
+                in_=src[:, :, lo:hi].rearrange("p j (c i) -> p c j i", i=LINE),
+            )
 
         for e in range(E):
             slots = slice(e * C, (e + 1) * C)
             acc = [psum.tile([P, C], F32, name="acc%d_%d" % (e, h)) for h in range(HALVES)]
             for o in range(PASSES):
-                grouped = []
+                grouped = ring.tile([P, N, PACK], BF16, name="grouped", align_bytes=64)
+                interleave(nc.vector.tensor_copy, grouped, raw[e, o], 0, SPLIT)
+                interleave(nc.scalar.copy, grouped, raw[e, o], SPLIT, N)
+                codes = keep.tile([P, N], U32, name="codes%d_%d" % (e, o), align_bytes=64)
+                scales = keep.tile([P, N], U8, name="scales%d_%d" % (e, o), align_bytes=64)
+                nc.vector.quantize_mx(
+                    out=codes[:].bitcast(FP8X4),
+                    scales=scales[:],
+                    in_=grouped[:].rearrange("p n j -> p (n j)"),
+                )
                 for h in range(HALVES):
-                    g = keep.tile([P, P, PACK], BF16, name="grouped%d_%d_%d" % (e, o, h), align_bytes=64)
-                    src = raw[e, o][:, :, h * P : (h + 1) * P].rearrange("p j (c i) -> p c j i", i=LINE)
-                    dst = g[:].rearrange("p (c i) j -> p c j i", i=LINE)
-                    if h == 0:
-                        nc.vector.tensor_copy(out=dst, in_=src)
-                    else:
-                        nc.scalar.copy(out=dst, in_=src)
-                    grouped.append(g)
-                for h in range(HALVES):
-                    codes = keep.tile([P, P], U32, name="codes%d_%d_%d" % (e, o, h), align_bytes=64)
-                    scales = keep.tile([P, P], U8, name="scales%d_%d_%d" % (e, o, h), align_bytes=64)
-                    nc.vector.quantize_mx(
-                        out=codes[:].bitcast(FP8X4),
-                        scales=scales[:],
-                        in_=grouped[h][:].rearrange("p n j -> p (n j)"),
-                    )
+                    cols = slice(h * P, (h + 1) * P)
                     nc.tensor.matmul_mx(
                         out=acc[h][:],
-                        lhsT=codes[:].bitcast(FP8X4),
-                        lhsT_scale=scales[:],
+                        lhsT=codes[:, cols].bitcast(FP8X4),
+                        lhsT_scale=scales[:, cols],
                         rhs=slot_words[o][:, slots].bitcast(FP8X4),
                         rhs_scale=slot_scales[4 * o : P, slots],
                         start=(o == 0),
                         stop=(o == PASSES - 1),
                     )
+            pos = keep.tile([P, HALVES, R, U], F32, name="pos%d" % e, align_bytes=64)
             for h in range(HALVES):
-                pos = keep.tile([P, R, U], F32, name="pos%d_%d" % (e, h), align_bytes=64)
                 nc.scalar.activation(
-                    out=pos[:].rearrange("p m u -> p (m u)"), in_=acc[h][:], func=ACT.Relu, bias=bias[:, h, e : e + 1]
+                    out=pos[:, h].rearrange("p m u -> p (m u)"), in_=acc[h][:], func=ACT.Relu, bias=bias[:, h, e : e + 1]
                 )
-                nc.vector.tensor_tensor(out=staged[h][:, :, e, :], in0=pos[:], in1=pos[:], op=ALU.mult)
+            nc.vector.tensor_tensor(out=staged[:, :, :, e, :], in0=pos[:], in1=pos[:], op=ALU.mult)
             if e == E - 2:
                 for h in range(HALVES):
-                    nc.sync.dma_start(out=out_view[h][:, :, 0 : E - 1, :], in_=staged[h][:, :, 0 : E - 1, :])
+                    nc.sync.dma_start(out=out_view[h][:, :, 0 : E - 1, :], in_=staged[:, h, :, 0 : E - 1, :])
         for h in range(HALVES):
-            nc.sync.dma_start(out=out_view[h][:, :, E - 1, :], in_=staged[h][:, :, E - 1, :])
+            nc.sync.dma_start(out=out_view[h][:, :, E - 1, :], in_=staged[:, h, :, E - 1, :])

@@ -23,6 +23,7 @@ HALVES = N // P
 U = C // R
 LINE = 4
 SPLIT = 96
+LAST_SPLIT = 176
 RING = 3
 
 
@@ -68,7 +69,7 @@ def tile_moe_pke_lin_relu2_kernel(tc, x_words, x_scales, w, b, offs, out):
         slot_scales = keep.tile([P, SLOTS], U8, name="slot_scales", align_bytes=64)
         nc.vector.tensor_copy(slot_scales[:], token_scales[:].indirect(offsets[:]))
 
-        staged = keep.tile([P, HALVES, R, E, U], F32, name="staged", align_bytes=64)
+        staged = keep.tile([P, HALVES, R, E - 1, U], F32, name="staged", align_bytes=64)
         out_view = out.rearrange("(h p) (m e u) -> h p m e u", p=P, m=R, e=E)
 
         def interleave(engine_copy, dst, src, lo, hi):
@@ -77,20 +78,30 @@ def tile_moe_pke_lin_relu2_kernel(tc, x_words, x_scales, w, b, offs, out):
                 in_=src[:, :, lo:hi].rearrange("p j (c i) -> p c j i", i=LINE),
             )
 
+        def quantise(codes, scales, grouped, lo, hi):
+            nc.vector.quantize_mx(
+                out=codes[:, lo:hi].bitcast(FP8X4),
+                scales=scales[:, lo:hi],
+                in_=grouped[:, lo:hi, :].rearrange("p n j -> p (n j)"),
+            )
+
         for e in range(E):
             slots = slice(e * C, (e + 1) * C)
             acc = [psum.tile([P, C], F32, name="acc%d_%d" % (e, h)) for h in range(HALVES)]
             for o in range(PASSES):
-                grouped = ring.tile([P, N, PACK], BF16, name="grouped", align_bytes=64)
-                interleave(nc.vector.tensor_copy, grouped, raw[e, o], 0, SPLIT)
-                interleave(nc.scalar.copy, grouped, raw[e, o], SPLIT, N)
                 codes = keep.tile([P, N], U32, name="codes%d_%d" % (e, o), align_bytes=64)
                 scales = keep.tile([P, N], U8, name="scales%d_%d" % (e, o), align_bytes=64)
-                nc.vector.quantize_mx(
-                    out=codes[:].bitcast(FP8X4),
-                    scales=scales[:],
-                    in_=grouped[:].rearrange("p n j -> p (n j)"),
-                )
+                grouped = ring.tile([P, N, PACK], BF16, name="grouped", align_bytes=64)
+                if (e, o) != (E - 1, PASSES - 1):
+                    interleave(nc.vector.tensor_copy, grouped, raw[e, o], 0, SPLIT)
+                    interleave(nc.scalar.copy, grouped, raw[e, o], SPLIT, N)
+                    quantise(codes, scales, grouped, 0, N)
+                else:
+                    interleave(nc.vector.tensor_copy, grouped, raw[e, o], 0, P)
+                    interleave(nc.vector.tensor_copy, grouped, raw[e, o], P, LAST_SPLIT)
+                    interleave(nc.scalar.copy, grouped, raw[e, o], LAST_SPLIT, N)
+                    for h in range(HALVES):
+                        quantise(codes, scales, grouped, h * P, (h + 1) * P)
                 for h in range(HALVES):
                     cols = slice(h * P, (h + 1) * P)
                     nc.tensor.matmul_mx(
@@ -102,14 +113,26 @@ def tile_moe_pke_lin_relu2_kernel(tc, x_words, x_scales, w, b, offs, out):
                         start=(o == 0),
                         stop=(o == PASSES - 1),
                     )
-            pos = keep.tile([P, HALVES, R, U], F32, name="pos%d" % e, align_bytes=64)
-            for h in range(HALVES):
-                nc.scalar.activation(
-                    out=pos[:, h].rearrange("p m u -> p (m u)"), in_=acc[h][:], func=ACT.Relu, bias=bias[:, h, e : e + 1]
+            if e < E - 1:
+                pos = keep.tile([P, HALVES, R, U], F32, name="pos%d" % e, align_bytes=64)
+                for h in range(HALVES):
+                    nc.scalar.activation(
+                        out=pos[:, h].rearrange("p m u -> p (m u)"), in_=acc[h][:], func=ACT.Relu, bias=bias[:, h, e : e + 1]
+                    )
+                nc.vector.tensor_tensor(out=staged[:, :, :, e, :], in0=pos[:], in1=pos[:], op=ALU.mult)
+            else:
+                pos = [keep.tile([P, C], F32, name="last_pos%d" % h, align_bytes=64) for h in range(HALVES)]
+                last = [keep.tile([P, R, U], F32, name="last%d" % h, align_bytes=64) for h in range(HALVES)]
+                nc.scalar.activation(out=pos[0][:], in_=acc[0][:], func=ACT.Relu, bias=bias[:, 0, e : e + 1])
+                nc.scalar.activation(out=last[0][:].rearrange("p m u -> p (m u)"), in_=pos[0][:], func=ACT.Square)
+                nc.vector.tensor_scalar(
+                    out=pos[1][:], in0=acc[1][:], scalar1=bias[:, 1, e : e + 1], scalar2=0.0, op0=ALU.add, op1=ALU.max
                 )
-            nc.vector.tensor_tensor(out=staged[:, :, :, e, :], in0=pos[:], in1=pos[:], op=ALU.mult)
+                nc.vector.tensor_tensor(
+                    out=last[1][:].rearrange("p m u -> p (m u)"), in0=pos[1][:], in1=pos[1][:], op=ALU.mult
+                )
+                nc.scalar.dma_start(out=out_view[0][:, :, e, :], in_=last[0][:])
+                nc.sync.dma_start(out=out_view[1][:, :, e, :], in_=last[1][:])
             if e == E - 2:
                 for h in range(HALVES):
-                    nc.sync.dma_start(out=out_view[h][:, :, 0 : E - 1, :], in_=staged[:, h, :, 0 : E - 1, :])
-        for h in range(HALVES):
-            nc.sync.dma_start(out=out_view[h][:, :, E - 1, :], in_=staged[:, h, :, E - 1, :])
+                    nc.sync.dma_start(out=out_view[h][:, :, 0 : E - 1, :], in_=staged[:, h])

@@ -21,7 +21,7 @@ PASSES = K // (P * PACK)
 SLOTS = E * C
 HALVES = N // P
 U = C // R
-LINE = 4
+LINE = 2
 SPLIT = 96
 LAST_SPLIT = 176
 RING = 3

@@ -24,6 +24,7 @@ U = C // R
 LINE = 2
 SPLIT = 96
 LAST_SPLIT = 176
+RAMP = {(E - 1, PASSES - 3): 128, (E - 1, PASSES - 2): 152}
 RING = 3
 
 
@@ -93,8 +94,9 @@ def tile_moe_pke_lin_relu2_kernel(tc, x_words, x_scales, w, b, offs, out):
                 scales = keep.tile([P, N], U8, name="scales%d_%d" % (e, o), align_bytes=64)
                 grouped = ring.tile([P, N, PACK], BF16, name="grouped", align_bytes=64)
                 if (e, o) != (E - 1, PASSES - 1):
-                    interleave(nc.vector.tensor_copy, grouped, raw[e, o], 0, SPLIT)
-                    interleave(nc.scalar.copy, grouped, raw[e, o], SPLIT, N)
+                    split = RAMP.get((e, o), SPLIT)
+                    interleave(nc.vector.tensor_copy, grouped, raw[e, o], 0, split)
+                    interleave(nc.scalar.copy, grouped, raw[e, o], split, N)
                     quantise(codes, scales, grouped, 0, N)
                 else:
                     interleave(nc.vector.tensor_copy, grouped, raw[e, o], 0, P)

@@ -26,6 +26,7 @@ SPLIT = 96
 LAST_SPLIT = 176
 RAMP = {(E - 1, PASSES - 3): 128, (E - 1, PASSES - 2): 152}
 RING = 3
+WARM = 2
 
 
 def tile_moe_pke_lin_relu2_kernel(tc, x_words, x_scales, w, b, offs, out):
@@ -88,7 +89,7 @@ def tile_moe_pke_lin_relu2_kernel(tc, x_words, x_scales, w, b, offs, out):
 
         for e in range(E):
             slots = slice(e * C, (e + 1) * C)
-            acc = [psum.tile([P, C], F32, name="acc%d_%d" % (e, h)) for h in range(HALVES)]
+            acc = [psum.tile([P, C], F32, name="acc%d_%d" % (e, h), tag="acc%d_%d" % (e, h)) for h in range(HALVES)]
             for o in range(PASSES):
                 codes = keep.tile([P, N], U32, name="codes%d_%d" % (e, o), align_bytes=64)
                 scales = keep.tile([P, N], U8, name="scales%d_%d" % (e, o), align_bytes=64)
@@ -114,6 +115,17 @@ def tile_moe_pke_lin_relu2_kernel(tc, x_words, x_scales, w, b, offs, out):
                         rhs_scale=slot_scales[4 * o : P, slots],
                         start=(o == 0),
                         stop=(o == PASSES - 1),
+                    )
+                if e == E - 1 and o < WARM:
+                    unread = psum.tile([P, SLOTS], F32, name="unread%d" % o, tag="acc0_%d" % o)
+                    nc.tensor.matmul_mx(
+                        out=unread[:],
+                        lhsT=codes[:, 0:P].bitcast(FP8X4),
+                        lhsT_scale=scales[:, 0:P],
+                        rhs=slot_words[o][:].bitcast(FP8X4),
+                        rhs_scale=slot_scales[4 * o : P, :],
+                        start=True,
+                        stop=True,
                     )
             if e < E - 1:
                 pos = keep.tile([P, HALVES, R, U], F32, name="pos%d" % e, align_bytes=64)

@@ -22,10 +22,13 @@ SLOTS = E * C
 HALVES = N // P
 U = C // R
 LINE = 2
-SPLIT = 96
+PIECES = E * PASSES
+SCALAR_PIECES = (0, 1, 2, 3, 4, 6, 8, 10)
+VECTOR_PIECES = (5, 7, 9, 11)
+BIAS_AFTER = 5
+SPLIT = 128
+NEXT_TO_LAST_SPLIT = 152
 LAST_SPLIT = 176
-RAMP = {(E - 1, PASSES - 3): 128, (E - 1, PASSES - 2): 152}
-RING = 3
 WARM = 2
 
 
@@ -33,35 +36,38 @@ def tile_moe_pke_lin_relu2_kernel(tc, x_words, x_scales, w, b, offs, out):
     nc = tc.nc
     with ExitStack() as ctx:
         keep = ctx.enter_context(tc.tile_pool(name="keep", bufs=1))
-        ring = ctx.enter_context(tc.tile_pool(name="ring", bufs=RING))
         psum = ctx.enter_context(tc.psum_pool(name="psum", bufs=1))
-
-        offsets = keep.tile([P, SLOTS // 16], U16, name="offsets")
-        nc.sync.dma_start(offsets[:], offs)
-
-        token_scales = keep.tile([P, T], U8, name="token_scales", align_bytes=64)
-        nc.vector.memset(token_scales[:].bitcast(I32), 0)
-        for q in range(4):
-            nc.scalar.dma_start(
-                out=token_scales[32 * q : 32 * q + 16, :].bitcast(I32),
-                in_=x_scales[:, 4 * q : 4 * q + 4, :].bitcast(I32),
-            )
-
-        bias = keep.tile([P, HALVES, E], F32, name="bias")
-        nc.scalar.dma_start(out=bias[:], in_=b.rearrange("(h p) e -> p h e", p=P))
 
         token_words = []
         for o in range(PASSES):
             words = keep.tile([P, T], I32, name="token_words%d" % o, align_bytes=64)
-            nc.sync.dma_start(out=words[:], in_=x_words[o].rearrange("p t r -> p (t r)").bitcast(I32))
+            nc.scalar.dma_start(out=words[:], in_=x_words[o].rearrange("p t r -> p (t r)").bitcast(I32))
             token_words.append(words)
 
+        offsets = keep.tile([P, SLOTS // 16], U16, name="offsets")
+        token_scales = keep.tile([P, T], U8, name="token_scales", align_bytes=64)
+        nc.vector.memset(token_scales[:].bitcast(I32), 0)
+        bias = keep.tile([P, HALVES, E], F32, name="bias")
+
+        def load_scale_rows(q):
+            nc.sync.dma_start(
+                out=token_scales[32 * q : 32 * q + 16, :].bitcast(I32),
+                in_=x_scales[:, 4 * q : 4 * q + 4, :].bitcast(I32),
+            )
+
         raw = {}
-        for e in range(E):
-            for o in range(PASSES):
-                raw[e, o] = keep.tile([P, PACK, N], F32, name="raw%d_%d" % (e, o), align_bytes=64)
-                rows = w[e, o * P * PACK : (o + 1) * P * PACK, :]
-                nc.sync.dma_start(out=raw[e, o][:], in_=rows.rearrange("(p j) n -> p j n", j=PACK))
+        for i in range(PIECES):
+            e, o = divmod(i, PASSES)
+            raw[e, o] = keep.tile([P, PACK, N], F32, name="raw%d" % i, align_bytes=64)
+            rows = w[e, o * P * PACK : (o + 1) * P * PACK, :]
+            nc.sync.dma_start(out=raw[e, o][:], in_=rows.rearrange("(p j) n -> p j n", j=PACK))
+            if i == 0:
+                nc.sync.dma_start(offsets[:], offs)
+            if i in (2, 3):
+                load_scale_rows(2 * (i - 2))
+                load_scale_rows(2 * (i - 2) + 1)
+            if i == BIAS_AFTER:
+                nc.sync.dma_start(out=bias[:], in_=b.rearrange("(h p) e -> p h e", p=P))
 
         slot_words = []
         for o in range(PASSES):
@@ -93,9 +99,16 @@ def tile_moe_pke_lin_relu2_kernel(tc, x_words, x_scales, w, b, offs, out):
             for o in range(PASSES):
                 codes = keep.tile([P, N], U32, name="codes%d_%d" % (e, o), align_bytes=64)
                 scales = keep.tile([P, N], U8, name="scales%d_%d" % (e, o), align_bytes=64)
-                grouped = ring.tile([P, N, PACK], BF16, name="grouped", align_bytes=64)
-                if (e, o) != (E - 1, PASSES - 1):
-                    split = RAMP.get((e, o), SPLIT)
+                i = e * PASSES + o
+                grouped = keep.tile([P, N, PACK], BF16, name="grouped%d" % i, align_bytes=64)
+                if i in SCALAR_PIECES:
+                    interleave(nc.scalar.copy, grouped, raw[e, o], 0, N)
+                    quantise(codes, scales, grouped, 0, N)
+                elif i in VECTOR_PIECES:
+                    interleave(nc.vector.tensor_copy, grouped, raw[e, o], 0, N)
+                    quantise(codes, scales, grouped, 0, N)
+                elif i < PIECES - 1:
+                    split = NEXT_TO_LAST_SPLIT if i == PIECES - 2 else SPLIT
                     interleave(nc.vector.tensor_copy, grouped, raw[e, o], 0, split)
                     interleave(nc.scalar.copy, grouped, raw[e, o], split, N)
                     quantise(codes, scales, grouped, 0, N)

@@ -24,12 +24,9 @@ U = C // R
 LINE = 2
 PIECES = E * PASSES
 SCALAR_PIECES = (0, 1, 2, 3, 4, 6, 8, 10)
-VECTOR_PIECES = (5, 7, 9, 11)
-BIAS_AFTER = 5
-SPLIT = 128
-NEXT_TO_LAST_SPLIT = 152
+VECTOR_PIECES = (5, 7, 9)
+SHARES = {11: 96, 12: 96, 13: 128, 14: 152}
 LAST_SPLIT = 176
-WARM = 2
 
 
 def tile_moe_pke_lin_relu2_kernel(tc, x_words, x_scales, w, b, offs, out):
@@ -38,36 +35,29 @@ def tile_moe_pke_lin_relu2_kernel(tc, x_words, x_scales, w, b, offs, out):
         keep = ctx.enter_context(tc.tile_pool(name="keep", bufs=1))
         psum = ctx.enter_context(tc.psum_pool(name="psum", bufs=1))
 
-        token_words = []
-        for o in range(PASSES):
-            words = keep.tile([P, T], I32, name="token_words%d" % o, align_bytes=64)
-            nc.scalar.dma_start(out=words[:], in_=x_words[o].rearrange("p t r -> p (t r)").bitcast(I32))
-            token_words.append(words)
-
-        offsets = keep.tile([P, SLOTS // 16], U16, name="offsets")
         token_scales = keep.tile([P, T], U8, name="token_scales", align_bytes=64)
         nc.vector.memset(token_scales[:].bitcast(I32), 0)
-        bias = keep.tile([P, HALVES, E], F32, name="bias")
-
-        def load_scale_rows(q):
-            nc.sync.dma_start(
+        for q in range(4):
+            nc.scalar.dma_start(
                 out=token_scales[32 * q : 32 * q + 16, :].bitcast(I32),
                 in_=x_scales[:, 4 * q : 4 * q + 4, :].bitcast(I32),
             )
+        bias = keep.tile([P, HALVES, E], F32, name="bias")
+        nc.scalar.dma_start(out=bias[:], in_=b.rearrange("(h p) e -> p h e", p=P))
 
+        offsets = keep.tile([P, SLOTS // 16], U16, name="offsets")
+        nc.sync.dma_start(offsets[:], offs)
+        token_words = []
         raw = {}
         for i in range(PIECES):
             e, o = divmod(i, PASSES)
+            if e == 0:
+                words = keep.tile([P, T], I32, name="token_words%d" % o, align_bytes=64)
+                nc.sync.dma_start(out=words[:], in_=x_words[o].rearrange("p t r -> p (t r)").bitcast(I32))
+                token_words.append(words)
             raw[e, o] = keep.tile([P, PACK, N], F32, name="raw%d" % i, align_bytes=64)
             rows = w[e, o * P * PACK : (o + 1) * P * PACK, :]
             nc.sync.dma_start(out=raw[e, o][:], in_=rows.rearrange("(p j) n -> p j n", j=PACK))
-            if i == 0:
-                nc.sync.dma_start(offsets[:], offs)
-            if i in (2, 3):
-                load_scale_rows(2 * (i - 2))
-                load_scale_rows(2 * (i - 2) + 1)
-            if i == BIAS_AFTER:
-                nc.sync.dma_start(out=bias[:], in_=b.rearrange("(h p) e -> p h e", p=P))
 
         slot_words = []
         for o in range(PASSES):
@@ -108,7 +98,7 @@ def tile_moe_pke_lin_relu2_kernel(tc, x_words, x_scales, w, b, offs, out):
                     interleave(nc.vector.tensor_copy, grouped, raw[e, o], 0, N)
                     quantise(codes, scales, grouped, 0, N)
                 elif i < PIECES - 1:
-                    split = NEXT_TO_LAST_SPLIT if i == PIECES - 2 else SPLIT
+                    split = SHARES[i]
                     interleave(nc.vector.tensor_copy, grouped, raw[e, o], 0, split)
                     interleave(nc.scalar.copy, grouped, raw[e, o], split, N)
                     quantise(codes, scales, grouped, 0, N)
@@ -128,17 +118,6 @@ def tile_moe_pke_lin_relu2_kernel(tc, x_words, x_scales, w, b, offs, out):
                         rhs_scale=slot_scales[4 * o : P, slots],
                         start=(o == 0),
                         stop=(o == PASSES - 1),
-                    )
-                if e == E - 1 and o < WARM:
-                    unread = psum.tile([P, SLOTS], F32, name="unread%d" % o, tag="acc0_%d" % o)
-                    nc.tensor.matmul_mx(
-                        out=unread[:],
-                        lhsT=codes[:, 0:P].bitcast(FP8X4),
-                        lhsT_scale=scales[:, 0:P],
-                        rhs=slot_words[o][:].bitcast(FP8X4),
-                        rhs_scale=slot_scales[4 * o : P, :],
-                        start=True,
-                        stop=True,
                     )
             if e < E - 1:
                 pos = keep.tile([P, HALVES, R, U], F32, name="pos%d" % e, align_bytes=64)

@@ -22,6 +22,7 @@ SLOTS = E * C
 HALVES = N // P
 U = C // R
 LINE = 2
+BURST = 256
 PIECES = E * PASSES
 SCALAR_PIECES = (0, 1, 2, 3, 4, 6, 8, 10)
 VECTOR_PIECES = (5, 7, 9)
@@ -35,27 +36,27 @@ def tile_moe_pke_lin_relu2_kernel(tc, x_words, x_scales, w, b, offs, out):
         keep = ctx.enter_context(tc.tile_pool(name="keep", bufs=1))
         psum = ctx.enter_context(tc.psum_pool(name="psum", bufs=1))
 
-        token_scales = keep.tile([P, T], U8, name="token_scales", align_bytes=64)
+        token_scales = keep.tile([P, T], U8, name="token_scales", align_bytes=BURST)
         nc.vector.memset(token_scales[:].bitcast(I32), 0)
         for q in range(4):
             nc.scalar.dma_start(
                 out=token_scales[32 * q : 32 * q + 16, :].bitcast(I32),
                 in_=x_scales[:, 4 * q : 4 * q + 4, :].bitcast(I32),
             )
-        bias = keep.tile([P, HALVES, E], F32, name="bias")
+        bias = keep.tile([P, HALVES, E], F32, name="bias", align_bytes=BURST)
         nc.scalar.dma_start(out=bias[:], in_=b.rearrange("(h p) e -> p h e", p=P))
 
-        offsets = keep.tile([P, SLOTS // 16], U16, name="offsets")
+        offsets = keep.tile([P, SLOTS // 16], U16, name="offsets", align_bytes=BURST)
         nc.sync.dma_start(offsets[:], offs)
         token_words = []
         raw = {}
         for i in range(PIECES):
             e, o = divmod(i, PASSES)
             if e == 0:
-                words = keep.tile([P, T], I32, name="token_words%d" % o, align_bytes=64)
+                words = keep.tile([P, T], I32, name="token_words%d" % o, align_bytes=BURST)
                 nc.sync.dma_start(out=words[:], in_=x_words[o].rearrange("p t r -> p (t r)").bitcast(I32))
                 token_words.append(words)
-            raw[e, o] = keep.tile([P, PACK, N], F32, name="raw%d" % i, align_bytes=64)
+            raw[e, o] = keep.tile([P, PACK, N], F32, name="raw%d" % i, align_bytes=BURST)
             rows = w[e, o * P * PACK : (o + 1) * P * PACK, :]
             nc.sync.dma_start(out=raw[e, o][:], in_=rows.rearrange("(p j) n -> p j n", j=PACK))
 

@@ -23,6 +23,7 @@ HALVES = N // P
 U = C // R
 LINE = 2
 BURST = 256
+ORDER = (1, 2, 3, 0)
 PIECES = E * PASSES
 SCALAR_PIECES = (0, 1, 2, 3, 4, 6, 8, 10)
 VECTOR_PIECES = (5, 7, 9)
@@ -51,8 +52,8 @@ def tile_moe_pke_lin_relu2_kernel(tc, x_words, x_scales, w, b, offs, out):
         token_words = []
         raw = {}
         for i in range(PIECES):
-            e, o = divmod(i, PASSES)
-            if e == 0:
+            e, o = ORDER[i // PASSES], i % PASSES
+            if i < PASSES:
                 words = keep.tile([P, T], I32, name="token_words%d" % o, align_bytes=BURST)
                 nc.sync.dma_start(out=words[:], in_=x_words[o].rearrange("p t r -> p (t r)").bitcast(I32))
                 token_words.append(words)
@@ -68,7 +69,7 @@ def tile_moe_pke_lin_relu2_kernel(tc, x_words, x_scales, w, b, offs, out):
         slot_scales = keep.tile([P, SLOTS], U8, name="slot_scales", align_bytes=64)
         nc.vector.tensor_copy(slot_scales[:], token_scales[:].indirect(offsets[:]))
 
-        staged = keep.tile([P, HALVES, R, E - 1, U], F32, name="staged", align_bytes=64)
+        staged = keep.tile([P, HALVES, R, E, U], F32, name="staged", align_bytes=BURST)
         out_view = out.rearrange("(h p) (m e u) -> h p m e u", p=P, m=R, e=E)
 
         def interleave(engine_copy, dst, src, lo, hi):
@@ -84,13 +85,13 @@ def tile_moe_pke_lin_relu2_kernel(tc, x_words, x_scales, w, b, offs, out):
                 in_=grouped[:, lo:hi, :].rearrange("p n j -> p (n j)"),
             )
 
-        for e in range(E):
+        for step, e in enumerate(ORDER):
             slots = slice(e * C, (e + 1) * C)
             acc = [psum.tile([P, C], F32, name="acc%d_%d" % (e, h), tag="acc%d_%d" % (e, h)) for h in range(HALVES)]
             for o in range(PASSES):
                 codes = keep.tile([P, N], U32, name="codes%d_%d" % (e, o), align_bytes=64)
                 scales = keep.tile([P, N], U8, name="scales%d_%d" % (e, o), align_bytes=64)
-                i = e * PASSES + o
+                i = step * PASSES + o
                 grouped = keep.tile([P, N, PACK], BF16, name="grouped%d" % i, align_bytes=64)
                 if i in SCALAR_PIECES:
                     interleave(nc.scalar.copy, grouped, raw[e, o], 0, N)
@@ -120,26 +121,25 @@ def tile_moe_pke_lin_relu2_kernel(tc, x_words, x_scales, w, b, offs, out):
                         start=(o == 0),
                         stop=(o == PASSES - 1),
                     )
-            if e < E - 1:
+            if step < E - 1:
                 pos = keep.tile([P, HALVES, R, U], F32, name="pos%d" % e, align_bytes=64)
                 for h in range(HALVES):
                     nc.scalar.activation(
                         out=pos[:, h].rearrange("p m u -> p (m u)"), in_=acc[h][:], func=ACT.Relu, bias=bias[:, h, e : e + 1]
                     )
-                nc.vector.tensor_tensor(out=staged[:, :, :, e, :], in0=pos[:], in1=pos[:], op=ALU.mult)
+                nc.vector.tensor_tensor(out=staged[:, :, :, step, :], in0=pos[:], in1=pos[:], op=ALU.mult)
             else:
-                pos = [keep.tile([P, C], F32, name="last_pos%d" % h, align_bytes=64) for h in range(HALVES)]
-                last = [keep.tile([P, R, U], F32, name="last%d" % h, align_bytes=64) for h in range(HALVES)]
-                nc.scalar.activation(out=pos[0][:], in_=acc[0][:], func=ACT.Relu, bias=bias[:, 0, e : e + 1])
-                nc.scalar.activation(out=last[0][:].rearrange("p m u -> p (m u)"), in_=pos[0][:], func=ACT.Square)
+                pos = [keep.tile([P, R, U], F32, name="last_pos%d" % h, align_bytes=64) for h in range(HALVES)]
+                last = [keep.tile([P, R, 2, U], F32, name="last%d" % h, align_bytes=BURST) for h in range(HALVES)]
+                flat = [pos[h][:].rearrange("p m u -> p (m u)") for h in range(HALVES)]
+                nc.scalar.activation(out=flat[0], in_=acc[0][:], func=ACT.Relu, bias=bias[:, 0, e : e + 1])
+                nc.scalar.activation(out=last[0][:, :, 0, :], in_=pos[0][:], func=ACT.Square)
                 nc.vector.tensor_scalar(
-                    out=pos[1][:], in0=acc[1][:], scalar1=bias[:, 1, e : e + 1], scalar2=0.0, op0=ALU.add, op1=ALU.max
+                    out=flat[1], in0=acc[1][:], scalar1=bias[:, 1, e : e + 1], scalar2=0.0, op0=ALU.add, op1=ALU.max
                 )
-                nc.vector.tensor_tensor(
-                    out=last[1][:].rearrange("p m u -> p (m u)"), in0=pos[1][:], in1=pos[1][:], op=ALU.mult
-                )
-                nc.scalar.dma_start(out=out_view[0][:, :, e, :], in_=last[0][:])
-                nc.sync.dma_start(out=out_view[1][:, :, e, :], in_=last[1][:])
-            if e == E - 2:
+                nc.vector.tensor_tensor(out=last[1][:, :, 0, :], in0=pos[1][:], in1=pos[1][:], op=ALU.mult)
+                nc.scalar.dma_start(out=out_view[0][:, :, e, :], in_=last[0][:, :, 0, :])
+                nc.sync.dma_start(out=out_view[1][:, :, e, :], in_=last[1][:, :, 0, :])
+            if step == E - 2:
                 for h in range(HALVES):
-                    nc.sync.dma_start(out=out_view[h][:, :, 0 : E - 1, :], in_=staged[:, h])
+                    nc.sync.dma_start(out=out_view[h][:, :, 1:E, :], in_=staged[:, h, :, 0 : E - 1, :])

@@ -38,14 +38,18 @@ def tile_moe_pke_lin_relu2_kernel(tc, x_words, x_scales, w, b, offs, out):
         psum = ctx.enter_context(tc.psum_pool(name="psum", bufs=1))
 
         token_scales = keep.tile([P, T], U8, name="token_scales", align_bytes=BURST)
-        nc.vector.memset(token_scales[:].bitcast(I32), 0)
+        upper_scales = keep.tile([P // 2, T], U8, name="upper_scales", align_bytes=BURST)
+        nc.vector.memset(token_scales[0 : P // 2, :].bitcast(I32), 0)
+        nc.vector.memset(upper_scales[:].bitcast(I32), 0)
         for q in range(4):
+            target = token_scales if q < 2 else upper_scales
             nc.scalar.dma_start(
-                out=token_scales[32 * q : 32 * q + 16, :].bitcast(I32),
+                out=target[32 * (q % 2) : 32 * (q % 2) + 16, :].bitcast(I32),
                 in_=x_scales[:, 4 * q : 4 * q + 4, :].bitcast(I32),
             )
-        bias = keep.tile([P, HALVES, E], F32, name="bias", align_bytes=BURST)
-        nc.scalar.dma_start(out=bias[:], in_=b.rearrange("(h p) e -> p h e", p=P))
+        nc.vector.tensor_copy(out=token_scales[P // 2 : P, :].bitcast(I32), in_=upper_scales[:].bitcast(I32))
+        bias = keep.tile([P, HALVES, 2 * E], F32, name="bias", align_bytes=BURST)
+        nc.scalar.dma_start(out=bias[:, :, 0:E], in_=b.rearrange("(h p) e -> p h e", p=P))
 
         offsets = keep.tile([P, SLOTS // 16], U16, name="offsets", align_bytes=BURST)
         nc.sync.dma_start(offsets[:], offs)

@@ -25,8 +25,8 @@ LINE = 2
 BURST = 256
 ORDER = (1, 2, 3, 0)
 PIECES = E * PASSES
-SCALAR_PIECES = (0, 1, 2, 3, 4, 6, 8, 10)
-VECTOR_PIECES = (5, 7, 9)
+SCALAR_PIECES = (0, 1, 2, 3, 10)
+PAIRED = (4, 6, 8)
 SHARES = {11: 96, 12: 96, 13: 128, 14: 152}
 LAST_SPLIT = 176
 
@@ -93,15 +93,25 @@ def tile_moe_pke_lin_relu2_kernel(tc, x_words, x_scales, w, b, offs, out):
             slots = slice(e * C, (e + 1) * C)
             acc = [psum.tile([P, C], F32, name="acc%d_%d" % (e, h), tag="acc%d_%d" % (e, h)) for h in range(HALVES)]
             for o in range(PASSES):
-                codes = keep.tile([P, N], U32, name="codes%d_%d" % (e, o), align_bytes=64)
-                scales = keep.tile([P, N], U8, name="scales%d_%d" % (e, o), align_bytes=64)
                 i = step * PASSES + o
-                grouped = keep.tile([P, N, PACK], BF16, name="grouped%d" % i, align_bytes=64)
-                if i in SCALAR_PIECES:
+                if i in PAIRED:
+                    both_codes = keep.tile([P, 2 * N], U32, name="codes%d" % i, align_bytes=64)
+                    both_scales = keep.tile([P, 2 * N], U8, name="scales%d" % i, align_bytes=64)
+                    both = keep.tile([P, 2 * N, PACK], BF16, name="grouped%d" % i, align_bytes=64)
+                    interleave(nc.scalar.copy, both[:, 0:N, :], raw[e, o], 0, N)
+                    interleave(nc.vector.tensor_copy, both[:, N : 2 * N, :], raw[e, o + 1], 0, N)
+                    quantise(both_codes, both_scales, both, 0, 2 * N)
+                    codes, scales = both_codes[:, 0:N], both_scales[:, 0:N]
+                elif i - 1 in PAIRED:
+                    codes, scales = both_codes[:, N : 2 * N], both_scales[:, N : 2 * N]
+                else:
+                    codes = keep.tile([P, N], U32, name="codes%d" % i, align_bytes=64)
+                    scales = keep.tile([P, N], U8, name="scales%d" % i, align_bytes=64)
+                    grouped = keep.tile([P, N, PACK], BF16, name="grouped%d" % i, align_bytes=64)
+                if i in PAIRED or i - 1 in PAIRED:
+                    pass
+                elif i in SCALAR_PIECES:
                     interleave(nc.scalar.copy, grouped, raw[e, o], 0, N)
-                    quantise(codes, scales, grouped, 0, N)
-                elif i in VECTOR_PIECES:
-                    interleave(nc.vector.tensor_copy, grouped, raw[e, o], 0, N)
                     quantise(codes, scales, grouped, 0, N)
                 elif i < PIECES - 1:
                     split = SHARES[i]

@@ -25,10 +25,11 @@ LINE = 2
 BURST = 256
 ORDER = (1, 2, 3, 0)
 PIECES = E * PASSES
+LAST = PIECES - 1
 SCALAR_PIECES = (0, 1, 2, 3, 10)
 PAIRED = (4, 6, 8)
-SHARES = {11: 96, 12: 96, 13: 128, 14: 152}
-LAST_SPLIT = 176
+SHARES = {11: 96, 12: 96, 13: 128, 14: 160}
+PARTS = ((0, 128, 80), (128, 256, 80))
 
 
 def tile_moe_pke_lin_relu2_kernel(tc, x_words, x_scales, w, b, offs, out):
@@ -54,16 +55,18 @@ def tile_moe_pke_lin_relu2_kernel(tc, x_words, x_scales, w, b, offs, out):
         offsets = keep.tile([P, SLOTS // 16], U16, name="offsets", align_bytes=BURST)
         nc.sync.dma_start(offsets[:], offs)
         token_words = []
-        raw = {}
+        raw = []
         for i in range(PIECES):
             e, o = ORDER[i // PASSES], i % PASSES
             if i < PASSES:
                 words = keep.tile([P, T], I32, name="token_words%d" % o, align_bytes=BURST)
                 nc.sync.dma_start(out=words[:], in_=x_words[o].rearrange("p t r -> p (t r)").bitcast(I32))
                 token_words.append(words)
-            raw[e, o] = keep.tile([P, PACK, N], F32, name="raw%d" % i, align_bytes=BURST)
-            rows = w[e, o * P * PACK : (o + 1) * P * PACK, :]
-            nc.sync.dma_start(out=raw[e, o][:], in_=rows.rearrange("(p j) n -> p j n", j=PACK))
+            rows = w[e, o * P * PACK : (o + 1) * P * PACK, :].rearrange("(p j) n -> p j n", j=PACK)
+            for lo, hi, mine in PARTS if i == LAST else ((0, N, 0),):
+                landed = keep.tile([P, PACK, hi - lo], F32, name="raw%d_%d" % (i, lo), align_bytes=BURST)
+                nc.sync.dma_start(out=landed[:], in_=rows[:, :, lo:hi])
+                raw.append(landed)
 
         slot_words = []
         for o in range(PASSES):
@@ -76,84 +79,106 @@ def tile_moe_pke_lin_relu2_kernel(tc, x_words, x_scales, w, b, offs, out):
         staged = keep.tile([P, HALVES, R, E, U], F32, name="staged", align_bytes=BURST)
         out_view = out.rearrange("(h p) (m e u) -> h p m e u", p=P, m=R, e=E)
 
-        def interleave(engine_copy, dst, src, lo, hi):
+        def interleave(engine_copy, dst, src):
             engine_copy(
-                out=dst[:, lo:hi, :].rearrange("p (c i) j -> p c j i", i=LINE),
-                in_=src[:, :, lo:hi].rearrange("p j (c i) -> p c j i", i=LINE),
+                out=dst.rearrange("p (c i) j -> p c j i", i=LINE),
+                in_=src.rearrange("p j (c i) -> p c j i", i=LINE),
             )
 
-        def quantise(codes, scales, grouped, lo, hi):
+        def share(dst, src, mine):
+            width = src.shape[2]
+            if mine > 0:
+                interleave(nc.vector.tensor_copy, dst[:, 0:mine, :], src[:, :, 0:mine])
+            if mine < width:
+                interleave(nc.scalar.copy, dst[:, mine:width, :], src[:, :, mine:width])
+
+        def quantise(tiles, lo, hi):
+            grouped, codes, scales = tiles
             nc.vector.quantize_mx(
                 out=codes[:, lo:hi].bitcast(FP8X4),
                 scales=scales[:, lo:hi],
                 in_=grouped[:, lo:hi, :].rearrange("p n j -> p (n j)"),
             )
 
-        for step, e in enumerate(ORDER):
+        def operand_tiles(i, width):
+            return (
+                keep.tile([P, width, PACK], BF16, name="grouped%d" % i, align_bytes=64),
+                keep.tile([P, width], U32, name="codes%d" % i, align_bytes=64),
+                keep.tile([P, width], U8, name="scales%d" % i, align_bytes=64),
+            )
+
+        acc = [
+            [psum.tile([P, C], F32, name="acc%d_%d" % (e, h), tag="acc%d_%d" % (e, h)) for h in range(HALVES)]
+            for e in range(E)
+        ]
+
+        def multiply(i, tiles, first, h):
+            e, o = ORDER[i // PASSES], i % PASSES
+            cols = slice(first + h * P, first + (h + 1) * P)
             slots = slice(e * C, (e + 1) * C)
-            acc = [psum.tile([P, C], F32, name="acc%d_%d" % (e, h), tag="acc%d_%d" % (e, h)) for h in range(HALVES)]
-            for o in range(PASSES):
-                i = step * PASSES + o
-                if i in PAIRED:
-                    both_codes = keep.tile([P, 2 * N], U32, name="codes%d" % i, align_bytes=64)
-                    both_scales = keep.tile([P, 2 * N], U8, name="scales%d" % i, align_bytes=64)
-                    both = keep.tile([P, 2 * N, PACK], BF16, name="grouped%d" % i, align_bytes=64)
-                    interleave(nc.scalar.copy, both[:, 0:N, :], raw[e, o], 0, N)
-                    interleave(nc.vector.tensor_copy, both[:, N : 2 * N, :], raw[e, o + 1], 0, N)
-                    quantise(both_codes, both_scales, both, 0, 2 * N)
-                    codes, scales = both_codes[:, 0:N], both_scales[:, 0:N]
-                elif i - 1 in PAIRED:
-                    codes, scales = both_codes[:, N : 2 * N], both_scales[:, N : 2 * N]
-                else:
-                    codes = keep.tile([P, N], U32, name="codes%d" % i, align_bytes=64)
-                    scales = keep.tile([P, N], U8, name="scales%d" % i, align_bytes=64)
-                    grouped = keep.tile([P, N, PACK], BF16, name="grouped%d" % i, align_bytes=64)
-                if i in PAIRED or i - 1 in PAIRED:
-                    pass
-                elif i in SCALAR_PIECES:
-                    interleave(nc.scalar.copy, grouped, raw[e, o], 0, N)
-                    quantise(codes, scales, grouped, 0, N)
-                elif i < PIECES - 1:
-                    split = SHARES[i]
-                    interleave(nc.vector.tensor_copy, grouped, raw[e, o], 0, split)
-                    interleave(nc.scalar.copy, grouped, raw[e, o], split, N)
-                    quantise(codes, scales, grouped, 0, N)
-                else:
-                    interleave(nc.vector.tensor_copy, grouped, raw[e, o], 0, P)
-                    interleave(nc.vector.tensor_copy, grouped, raw[e, o], P, LAST_SPLIT)
-                    interleave(nc.scalar.copy, grouped, raw[e, o], LAST_SPLIT, N)
-                    for h in range(HALVES):
-                        quantise(codes, scales, grouped, h * P, (h + 1) * P)
-                for h in range(HALVES):
-                    cols = slice(h * P, (h + 1) * P)
-                    nc.tensor.matmul_mx(
-                        out=acc[h][:],
-                        lhsT=codes[:, cols].bitcast(FP8X4),
-                        lhsT_scale=scales[:, cols],
-                        rhs=slot_words[o][:, slots].bitcast(FP8X4),
-                        rhs_scale=slot_scales[4 * o : P, slots],
-                        start=(o == 0),
-                        stop=(o == PASSES - 1),
-                    )
-            if step < E - 1:
+            nc.tensor.matmul_mx(
+                out=acc[e][h][:],
+                lhsT=tiles[1][:, cols].bitcast(FP8X4),
+                lhsT_scale=tiles[2][:, cols],
+                rhs=slot_words[o][:, slots].bitcast(FP8X4),
+                rhs_scale=slot_scales[4 * o : P, slots],
+                start=(o == 0),
+                stop=(o == PASSES - 1),
+            )
+
+        for i in range(LAST - 1):
+            step = i // PASSES
+            if i in PAIRED:
+                tiles = operand_tiles(i, 2 * N)
+                share(tiles[0][:, 0:N, :], raw[i][:], 0)
+                share(tiles[0][:, N : 2 * N, :], raw[i + 1][:], N)
+                quantise(tiles, 0, 2 * N)
+            elif i - 1 not in PAIRED:
+                tiles = operand_tiles(i, N)
+                share(tiles[0][:], raw[i][:], 0 if i in SCALAR_PIECES else SHARES[i])
+                quantise(tiles, 0, N)
+            for h in range(HALVES):
+                multiply(i, tiles, N if i - 1 in PAIRED else 0, h)
+            if i % PASSES == PASSES - 1:
+                e = ORDER[step]
                 pos = keep.tile([P, HALVES, R, U], F32, name="pos%d" % e, align_bytes=64)
                 for h in range(HALVES):
                     nc.scalar.activation(
-                        out=pos[:, h].rearrange("p m u -> p (m u)"), in_=acc[h][:], func=ACT.Relu, bias=bias[:, h, e : e + 1]
+                        out=pos[:, h].rearrange("p m u -> p (m u)"), in_=acc[e][h][:], func=ACT.Relu, bias=bias[:, h, e : e + 1]
                     )
                 nc.vector.tensor_tensor(out=staged[:, :, :, step, :], in0=pos[:], in1=pos[:], op=ALU.mult)
-            else:
-                pos = [keep.tile([P, R, U], F32, name="last_pos%d" % h, align_bytes=64) for h in range(HALVES)]
-                last = [keep.tile([P, R, 2, U], F32, name="last%d" % h, align_bytes=BURST) for h in range(HALVES)]
-                flat = [pos[h][:].rearrange("p m u -> p (m u)") for h in range(HALVES)]
-                nc.scalar.activation(out=flat[0], in_=acc[0][:], func=ACT.Relu, bias=bias[:, 0, e : e + 1])
-                nc.scalar.activation(out=last[0][:, :, 0, :], in_=pos[0][:], func=ACT.Square)
-                nc.vector.tensor_scalar(
-                    out=flat[1], in0=acc[1][:], scalar1=bias[:, 1, e : e + 1], scalar2=0.0, op0=ALU.add, op1=ALU.max
-                )
-                nc.vector.tensor_tensor(out=last[1][:, :, 0, :], in0=pos[1][:], in1=pos[1][:], op=ALU.mult)
-                nc.scalar.dma_start(out=out_view[0][:, :, e, :], in_=last[0][:, :, 0, :])
-                nc.sync.dma_start(out=out_view[1][:, :, e, :], in_=last[1][:, :, 0, :])
-            if step == E - 2:
-                for h in range(HALVES):
-                    nc.sync.dma_start(out=out_view[h][:, :, 1:E, :], in_=staged[:, h, :, 0 : E - 1, :])
+                if step == E - 2:
+                    for h in range(HALVES):
+                        nc.sync.dma_start(out=out_view[h][:, :, 1:E, :], in_=staged[:, h, :, 0 : E - 1, :])
+
+        e = ORDER[E - 1]
+        before = operand_tiles(LAST - 1, N)
+        final = operand_tiles(LAST, N)
+        pos = [keep.tile([P, R, U], F32, name="last_pos%d" % h, align_bytes=64) for h in range(HALVES)]
+        last = [keep.tile([P, R, 2, U], F32, name="last%d" % h, align_bytes=BURST) for h in range(HALVES)]
+        flat = [pos[h][:].rearrange("p m u -> p (m u)") for h in range(HALVES)]
+
+        def copy_part(k):
+            lo, hi, mine = PARTS[k]
+            share(final[0][:, lo:hi, :], raw[LAST + k][:], mine)
+
+        share(before[0][:], raw[LAST - 1][:], SHARES[LAST - 1])
+        copy_part(0)
+        quantise(before, 0, N)
+        for h in range(HALVES):
+            multiply(LAST - 1, before, 0, h)
+        quantise(final, 0, P)
+        multiply(LAST, final, 0, 0)
+        for k in range(1, len(PARTS)):
+            copy_part(k)
+        for k in range(1, len(PARTS)):
+            quantise(final, PARTS[k][0], PARTS[k][1])
+        multiply(LAST, final, 0, 1)
+        nc.scalar.activation(out=flat[0], in_=acc[e][0][:], func=ACT.Relu, bias=bias[:, 0, e : e + 1])
+        nc.scalar.activation(out=last[0][:, :, 0, :], in_=pos[0][:], func=ACT.Square)
+        nc.scalar.dma_start(out=out_view[0][:, :, e, :], in_=last[0][:, :, 0, :])
+        nc.vector.tensor_scalar(
+            out=flat[1], in0=acc[e][1][:], scalar1=bias[:, 1, e : e + 1], scalar2=0.0, op0=ALU.add, op1=ALU.max
+        )
+        nc.vector.tensor_tensor(out=last[1][:, :, 0, :], in0=pos[1][:], in1=pos[1][:], op=ALU.mult)
+        nc.sync.dma_start(out=out_view[1][:, :, e, :], in_=last[1][:, :, 0, :])

@@ -26,10 +26,9 @@ BURST = 256
 ORDER = (1, 2, 3, 0)
 PIECES = E * PASSES
 LAST = PIECES - 1
-SCALAR_PIECES = (0, 1, 2, 3, 10)
-PAIRED = (4, 6, 8)
-SHARES = {11: 96, 12: 96, 13: 128, 14: 160}
-PARTS = ((0, 128, 80), (128, 256, 80))
+SCALAR_PIECES = (0, 1, 2, 3, 4, 6, 8, 10)
+SHARES = {5: 256, 7: 256, 9: 256, 11: 96, 12: 96, 13: 128, 14: 136}
+PARTS = ((0, 128, 64), (128, 256, 80))
 
 
 def tile_moe_pke_lin_relu2_kernel(tc, x_words, x_scales, w, b, offs, out):
@@ -128,17 +127,11 @@ def tile_moe_pke_lin_relu2_kernel(tc, x_words, x_scales, w, b, offs, out):
 
         for i in range(LAST - 1):
             step = i // PASSES
-            if i in PAIRED:
-                tiles = operand_tiles(i, 2 * N)
-                share(tiles[0][:, 0:N, :], raw[i][:], 0)
-                share(tiles[0][:, N : 2 * N, :], raw[i + 1][:], N)
-                quantise(tiles, 0, 2 * N)
-            elif i - 1 not in PAIRED:
-                tiles = operand_tiles(i, N)
-                share(tiles[0][:], raw[i][:], 0 if i in SCALAR_PIECES else SHARES[i])
-                quantise(tiles, 0, N)
+            tiles = operand_tiles(i, N)
+            share(tiles[0][:], raw[i][:], 0 if i in SCALAR_PIECES else SHARES[i])
+            quantise(tiles, 0, N)
             for h in range(HALVES):
-                multiply(i, tiles, N if i - 1 in PAIRED else 0, h)
+                multiply(i, tiles, 0, h)
             if i % PASSES == PASSES - 1:
                 e = ORDER[step]
                 pos = keep.tile([P, HALVES, R, U], F32, name="pos%d" % e, align_bytes=64)

from contextlib import ExitStack

import concourse.mybir as mybir

K, T, E, C, N, R = 2048, 1024, 4, 128, 256, 4
FLOPS = 2 * K * N * E * C

F32 = mybir.dt.float32
BF16 = mybir.dt.bfloat16
I32 = mybir.dt.int32
U32 = mybir.dt.uint32
U16 = mybir.dt.uint16
U8 = mybir.dt.uint8
FP8X4 = mybir.dt.float8_e4m3fn_x4
ACT = mybir.ActivationFunctionType
ALU = mybir.AluOpType

P = 128
PACK = 4
PASSES = K // (P * PACK)
SLOTS = E * C
HALVES = N // P
U = C // R
LINE = 2
BURST = 256
ORDER = (1, 2, 3, 0)
PIECES = E * PASSES
LAST = PIECES - 1
SCALAR_PIECES = (0, 1, 2, 3, 4, 6, 8, 10)
SHARES = {5: 256, 7: 256, 9: 256, 11: 96, 12: 96, 13: 128, 14: 136}
PARTS = ((0, 128, 64), (128, 256, 80))


def tile_moe_pke_lin_relu2_kernel(tc, x_words, x_scales, w, b, offs, out):
    nc = tc.nc
    with ExitStack() as ctx:
        keep = ctx.enter_context(tc.tile_pool(name="keep", bufs=1))
        psum = ctx.enter_context(tc.psum_pool(name="psum", bufs=1))

        token_scales = keep.tile([P, T], U8, name="token_scales", align_bytes=BURST)
        upper_scales = keep.tile([P // 2, T], U8, name="upper_scales", align_bytes=BURST)
        nc.vector.memset(token_scales[0 : P // 2, :].bitcast(I32), 0)
        nc.vector.memset(upper_scales[:].bitcast(I32), 0)
        for q in range(4):
            target = token_scales if q < 2 else upper_scales
            nc.scalar.dma_start(
                out=target[32 * (q % 2) : 32 * (q % 2) + 16, :].bitcast(I32),
                in_=x_scales[:, 4 * q : 4 * q + 4, :].bitcast(I32),
            )
        nc.vector.tensor_copy(out=token_scales[P // 2 : P, :].bitcast(I32), in_=upper_scales[:].bitcast(I32))
        bias = keep.tile([P, HALVES, 2 * E], F32, name="bias", align_bytes=BURST)
        nc.scalar.dma_start(out=bias[:, :, 0:E], in_=b.rearrange("(h p) e -> p h e", p=P))

        offsets = keep.tile([P, SLOTS // 16], U16, name="offsets", align_bytes=BURST)
        nc.sync.dma_start(offsets[:], offs)
        token_words = []
        raw = []
        for i in range(PIECES):
            e, o = ORDER[i // PASSES], i % PASSES
            if i < PASSES:
                words = keep.tile([P, T], I32, name="token_words%d" % o, align_bytes=BURST)
                nc.sync.dma_start(out=words[:], in_=x_words[o].rearrange("p t r -> p (t r)").bitcast(I32))
                token_words.append(words)
            rows = w[e, o * P * PACK : (o + 1) * P * PACK, :].rearrange("(p j) n -> p j n", j=PACK)
            for lo, hi, mine in PARTS if i == LAST else ((0, N, 0),):
                landed = keep.tile([P, PACK, hi - lo], F32, name="raw%d_%d" % (i, lo), align_bytes=BURST)
                nc.sync.dma_start(out=landed[:], in_=rows[:, :, lo:hi])
                raw.append(landed)

        slot_words = []
        for o in range(PASSES):
            gathered = keep.tile([P, SLOTS], U32, name="slot_words%d" % o, align_bytes=64)
            nc.vector.tensor_copy(gathered[:], token_words[o][:].bitcast(U32).indirect(offsets[:]))
            slot_words.append(gathered)
        slot_scales = keep.tile([P, SLOTS], U8, name="slot_scales", align_bytes=64)
        nc.vector.tensor_copy(slot_scales[:], token_scales[:].indirect(offsets[:]))

        staged = keep.tile([P, HALVES, R, E, U], F32, name="staged", align_bytes=BURST)
        out_view = out.rearrange("(h p) (m e u) -> h p m e u", p=P, m=R, e=E)

        def interleave(engine_copy, dst, src):
            engine_copy(
                out=dst.rearrange("p (c i) j -> p c j i", i=LINE),
                in_=src.rearrange("p j (c i) -> p c j i", i=LINE),
            )

        def share(dst, src, mine):
            width = src.shape[2]
            if mine > 0:
                interleave(nc.vector.tensor_copy, dst[:, 0:mine, :], src[:, :, 0:mine])
            if mine < width:
                interleave(nc.scalar.copy, dst[:, mine:width, :], src[:, :, mine:width])

        def quantise(tiles, lo, hi):
            grouped, codes, scales = tiles
            nc.vector.quantize_mx(
                out=codes[:, lo:hi].bitcast(FP8X4),
                scales=scales[:, lo:hi],
                in_=grouped[:, lo:hi, :].rearrange("p n j -> p (n j)"),
            )

        def operand_tiles(i, width):
            return (
                keep.tile([P, width, PACK], BF16, name="grouped%d" % i, align_bytes=64),
                keep.tile([P, width], U32, name="codes%d" % i, align_bytes=64),
                keep.tile([P, width], U8, name="scales%d" % i, align_bytes=64),
            )

        acc = [
            [psum.tile([P, C], F32, name="acc%d_%d" % (e, h), tag="acc%d_%d" % (e, h)) for h in range(HALVES)]
            for e in range(E)
        ]

        def multiply(i, tiles, first, h):
            e, o = ORDER[i // PASSES], i % PASSES
            cols = slice(first + h * P, first + (h + 1) * P)
            slots = slice(e * C, (e + 1) * C)
            nc.tensor.matmul_mx(
                out=acc[e][h][:],
                lhsT=tiles[1][:, cols].bitcast(FP8X4),
                lhsT_scale=tiles[2][:, cols],
                rhs=slot_words[o][:, slots].bitcast(FP8X4),
                rhs_scale=slot_scales[4 * o : P, slots],
                start=(o == 0),
                stop=(o == PASSES - 1),
            )

        for i in range(LAST - 1):
            step = i // PASSES
            tiles = operand_tiles(i, N)
            share(tiles[0][:], raw[i][:], 0 if i in SCALAR_PIECES else SHARES[i])
            quantise(tiles, 0, N)
            for h in range(HALVES):
                multiply(i, tiles, 0, h)
            if i % PASSES == PASSES - 1:
                e = ORDER[step]
                pos = keep.tile([P, HALVES, R, U], F32, name="pos%d" % e, align_bytes=64)
                for h in range(HALVES):
                    nc.scalar.activation(
                        out=pos[:, h].rearrange("p m u -> p (m u)"), in_=acc[e][h][:], func=ACT.Relu, bias=bias[:, h, e : e + 1]
                    )
                nc.vector.tensor_tensor(out=staged[:, :, :, step, :], in0=pos[:], in1=pos[:], op=ALU.mult)
                if step == E - 2:
                    for h in range(HALVES):
                        nc.sync.dma_start(out=out_view[h][:, :, 1:E, :], in_=staged[:, h, :, 0 : E - 1, :])

        e = ORDER[E - 1]
        before = operand_tiles(LAST - 1, N)
        final = operand_tiles(LAST, N)
        pos = [keep.tile([P, R, U], F32, name="last_pos%d" % h, align_bytes=64) for h in range(HALVES)]
        last = [keep.tile([P, R, 2, U], F32, name="last%d" % h, align_bytes=BURST) for h in range(HALVES)]
        flat = [pos[h][:].rearrange("p m u -> p (m u)") for h in range(HALVES)]

        def copy_part(k):
            lo, hi, mine = PARTS[k]
            share(final[0][:, lo:hi, :], raw[LAST + k][:], mine)

        share(before[0][:], raw[LAST - 1][:], SHARES[LAST - 1])
        copy_part(0)
        quantise(before, 0, N)
        for h in range(HALVES):
            multiply(LAST - 1, before, 0, h)
        quantise(final, 0, P)
        multiply(LAST, final, 0, 0)
        for k in range(1, len(PARTS)):
            copy_part(k)
        for k in range(1, len(PARTS)):
            quantise(final, PARTS[k][0], PARTS[k][1])
        multiply(LAST, final, 0, 1)
        nc.scalar.activation(out=flat[0], in_=acc[e][0][:], func=ACT.Relu, bias=bias[:, 0, e : e + 1])
        nc.scalar.activation(out=last[0][:, :, 0, :], in_=pos[0][:], func=ACT.Square)
        nc.scalar.dma_start(out=out_view[0][:, :, e, :], in_=last[0][:, :, 0, :])
        nc.vector.tensor_scalar(
            out=flat[1], in0=acc[e][1][:], scalar1=bias[:, 1, e : e + 1], scalar2=0.0, op0=ALU.add, op1=ALU.max
        )
        nc.vector.tensor_tensor(out=last[1][:, :, 0, :], in0=pos[1][:], in1=pos[1][:], op=ALU.mult)
        nc.sync.dma_start(out=out_view[1][:, :, e, :], in_=last[1][:, :, 0, :])
